import numpy as np
import ml_dtypes


def mxq(x, axis, fmt="e4m3"):
    dtype, down = {"e4m3": (ml_dtypes.float8_e4m3fn, 7), "e5m2": (ml_dtypes.float8_e5m2, 14)}[fmt]
    v = np.moveaxis(np.asarray(x, np.float32).astype(ml_dtypes.bfloat16).astype(np.float64), axis, -1)
    blocks = v.reshape(v.shape[:-1] + (-1, 32))
    amax = np.abs(blocks).max(-1, keepdims=True)
    byte = np.maximum(np.where(amax > 0, np.frexp(amax)[1] - 1 + 127, 0) - down, 1)
    scale = np.exp2(byte - 127.0)
    codes = (blocks / scale).astype(np.float32).astype(dtype).astype(np.float64)
    return np.moveaxis((codes * scale).reshape(v.shape), -1, axis)


WIDE = False


def mx_kscale(k):
    if not WIDE:
        return np.ones(k)
    levels = np.array([10, -10, 5, -5, 0])
    if k % 512:
        return np.exp2(np.random.permutation(np.resize(levels, k // 32))).repeat(32)
    a = np.empty((k // 512, 16))
    for p in range(k // 512):
        a[p, :8] = np.random.permutation(np.resize(levels, 8))
        for g in range(8):
            far = levels[np.abs(levels - a[p, g]) >= 10]
            a[p, g + 8] = far[np.random.randint(len(far))]
    return np.exp2(a.ravel()).repeat(32)


def f64(x):
    return np.asarray(x).astype(np.float64)


def striped8(idx):
    return np.asarray(idx).reshape(8, -1, 16).transpose(0, 2, 1).reshape(128, -1).astype(np.uint16)


def unstriped8(offs):
    return offs.reshape(8, 16, -1).transpose(0, 2, 1).reshape(8, -1).astype(np.int64)


def pick8(x, idx, run):
    r = np.arange(len(x))
    return x[r[:, None], idx[r % (8 * run) // run]]


E2M1 = np.array([0.0, 0.5, 1.0, 1.5, 2.0, 3.0, 4.0, 6.0, -0.0, -0.5, -1.0, -1.5, -2.0, -3.0, -4.0, -6.0])


def pack_weight(w, fmt):
    k, n = w.shape
    w = f64(np.asarray(w, np.float32).astype(ml_dtypes.bfloat16)).reshape(k // 32, 32, n)
    amax = np.abs(w).max(1)
    if fmt == "e4m3":
        byte = np.frexp(amax)[1] - 1 + 127 - 7
    else:
        mant, ex = np.frexp(amax / 6.0)
        byte = np.where(mant > 0.5, ex, ex - 1) + 127
    byte = np.clip(np.where(amax > 0, byte, 1), 1, 254)
    scaled = (w * np.exp2(127.0 - byte)[:, None, :]).reshape(k, n).astype(np.float32)
    by_word = np.ascontiguousarray(scaled.reshape(k // 512, 128, 4, n).transpose(0, 1, 3, 2))
    if fmt == "e4m3":
        words = by_word.astype(ml_dtypes.float8_e4m3fn).view(np.uint8)
    else:
        c = by_word.astype(ml_dtypes.float4_e2m1fn).view(np.uint8) & 0xF
        words = (c[..., 0::2] | (c[..., 1::2] << 4)).reshape(k // 512, 128, 2 * n)
    return np.ascontiguousarray(words), np.ascontiguousarray(byte.astype(np.uint8).reshape(k // 512, 16, n))


def unpack_weight(words, scales, fmt):
    g, _, n = scales.shape
    words = np.ascontiguousarray(words).reshape(g, 128, n, -1)
    if fmt == "e4m3":
        vals = words.view(ml_dtypes.float8_e4m3fn).astype(np.float64)
    else:
        nib = np.empty((g, 128, n, 4), np.uint8)
        nib[..., 0::2] = words & 0xF
        nib[..., 1::2] = words >> 4
        vals = E2M1[nib]
    vals = vals * np.repeat(np.exp2(scales.astype(np.float64) - 127.0), 8, axis=1)[..., None]
    return vals.transpose(0, 1, 3, 2).reshape(g * 512, n)


D, T, I, Q = 512, 1024, 512, 128


def setup_inputs():
    n = np.random.standard_normal
    idx = np.stack([np.random.permutation(T)[:I] for _ in range(8)])
    idx2 = np.stack([np.random.permutation(T)[:I] for _ in range(8)])
    idx3 = np.stack([np.random.permutation(T)[:I] for _ in range(8)])
    idx4 = np.stack([np.random.permutation(T)[:I] for _ in range(8)])
    fd = mx_kscale(D)
    keysp = pack_weight(n((D, T)) / fd[:, None], "e4m3")
    return {
        "query": (n((D, Q)) * 1.0 / np.sqrt(D) * fd[:, None]).astype(np.float32),
        "keys_words": keysp[0],
        "keys_scales": keysp[1],
        "old": (1.0 * n((Q, T))).astype(np.float32),
        "offs": striped8(idx),
        "offs2": striped8(idx2),
        "offs3": striped8(idx3),
        "offs4": striped8(idx4),
    }


def reference(query, keys_words, keys_scales, old, offs, offs2, offs3, offs4):
    idx = unstriped8(offs)
    idx2 = unstriped8(offs2)
    idx3 = unstriped8(offs3)
    idx4 = unstriped8(offs4)
    keysu = unpack_weight(keys_words, keys_scales, "e4m3")
    queryq = mxq(f64(query), 0, "e4m3")
    a = queryq.T @ keysu
    w = pick8(a, idx, 16) - pick8(a, idx2, 16)
    f1 = np.zeros((Q, T))
    f1[np.arange(Q)[:, None], idx[np.arange(Q) % 128 // 16]] = w
    f2 = f1 + f64(old)
    y = np.maximum(pick8(f2, idx3, 16), pick8(f2, idx4, 16))
    return y

@@ -1,0 +1,117 @@
+from contextlib import ExitStack
+
+import concourse.mybir as mybir
+
+D, T, I, Q = 512, 1024, 512, 128
+FLOPS = 2 * D * T * Q
+
+F32 = mybir.dt.float32
+BF16 = mybir.dt.bfloat16
+I32 = mybir.dt.int32
+U32 = mybir.dt.uint32
+U16 = mybir.dt.uint16
+U8 = mybir.dt.uint8
+FP8X4 = mybir.dt.float8_e4m3fn_x4
+COPY = mybir.ActivationFunctionType.Copy
+ADD = mybir.AluOpType.add
+MAX = mybir.AluOpType.max
+
+P = 128
+PACK = 4
+GROUP = 16
+HALF = I // 2
+KEY_LOADS = 2
+N_MM = 256
+
+
+def tile_attend_difference_lean_throughtwo_heads_kernel(
+    tc, query, keys_words, keys_scales, old, offs, offs2, offs3, offs4, out
+):
+    nc = tc.nc
+    with ExitStack() as ctx:
+        lists = ctx.enter_context(tc.tile_pool(name="lists", bufs=1))
+        sb = ctx.enter_context(tc.tile_pool(name="sb", bufs=1))
+        psum = ctx.enter_context(tc.psum_pool(name="psum", bufs=1))
+
+        k_scales = sb.tile([P, T], U8, name="k_scales", align_bytes=64)
+        nc.vector.memset(k_scales[:].bitcast(I32), 0)
+
+        q_raw = sb.tile([P, PACK, Q], F32, name="q_raw", tag="staged")
+        nc.sync.dma_start(out=q_raw[:], in_=query.rearrange("(p j) q -> p j q", j=PACK))
+
+        words = keys_words[0].rearrange("p t r -> p (t r)").bitcast(I32)
+        width = T // KEY_LOADS
+        k_words = [sb.tile([P, width], U32, name="k_words%d" % c, align_bytes=64) for c in range(KEY_LOADS)]
+        nc.sync.dma_start(out=k_words[0][:].bitcast(I32), in_=words[:, 0:width])
+        scale_rows = keys_scales[0].bitcast(I32)
+        for quad in range(4):
+            nc.sync.dma_start(
+                out=k_scales[32 * quad : 32 * quad + 4, :].bitcast(I32),
+                in_=scale_rows[4 * quad : 4 * quad + 4, :],
+            )
+        nc.sync.dma_start(out=k_words[1][:].bitcast(I32), in_=words[:, width:T])
+
+        idx = lists.tile([P, I // GROUP], U16, name="idx")
+        idx2 = lists.tile([P, I // GROUP], U16, name="idx2")
+        idx3 = lists.tile([P, I // GROUP], U16, name="idx3")
+        idx4 = lists.tile([P, I // GROUP], U16, name="idx4")
+        nc.sync.dma_start(idx[:], offs)
+        nc.sync.dma_start(idx2[:], offs2)
+
+        f1 = sb.tile([P, T], F32, name="f1")
+        nc.vector.memset(f1[:], 0.0)
+
+        q_bf = sb.tile([P, Q, PACK], BF16, name="q_bf", align_bytes=64)
+        nc.vector.tensor_copy(out=q_bf[:], in_=q_raw[:].rearrange("p j q -> p q j"))
+        q_words = sb.tile([P, Q], U32, name="q_words", align_bytes=64)
+        q_scales = sb.tile([P, Q], U8, name="q_scales", align_bytes=64)
+        nc.vector.quantize_mx(
+            out=q_words[:].bitcast(FP8X4), scales=q_scales[:], in_=q_bf[:].rearrange("p q j -> p (q j)")
+        )
+
+        old_sb = sb.tile([P, T], F32, name="old_sb", tag="staged")
+        nc.sync.dma_start(out=old_sb[:], in_=old)
+        nc.sync.dma_start(idx3[:], offs3)
+        nc.sync.dma_start(idx4[:], offs4)
+
+        a = sb.tile([P, T], F32, name="a")
+        for m in range(T // N_MM):
+            cols = slice(m * N_MM, (m + 1) * N_MM)
+            c, first = divmod(m * N_MM, width)
+            bank = psum.tile([P, N_MM], F32, name="bank%d" % m)
+            nc.tensor.matmul_mx(
+                out=bank[:],
+                lhsT=q_words[:].bitcast(FP8X4),
+                lhsT_scale=q_scales[:],
+                rhs=k_words[c][:, first : first + N_MM].bitcast(FP8X4),
+                rhs_scale=k_scales[:, cols],
+                start=True,
+                stop=True,
+            )
+            if m % 2 == 0:
+                nc.scalar.activation(a[:, cols], bank[:], COPY)
+            else:
+                nc.vector.tensor_copy(a[:, cols], bank[:])
+
+        halves = [slice(h * HALF // GROUP, (h + 1) * HALF // GROUP) for h in range(2)]
+        plus = [sb.tile([P, HALF], F32, name="plus%d" % h) for h in range(2)]
+        minus = [sb.tile([P, HALF], F32, name="minus%d" % h) for h in range(2)]
+        nc.vector.tensor_copy(plus[0][:], a[:].indirect(idx[:, halves[0]]))
+        nc.scalar.activation(minus[0][:], a[:].indirect(idx2[:, halves[0]]), COPY, scale=-1.0)
+        nc.scalar.activation(plus[1][:], a[:].indirect(idx[:, halves[1]]), COPY)
+        nc.scalar.activation(minus[1][:], a[:].indirect(idx2[:, halves[1]]), COPY, scale=-1.0)
+        for h in range(2):
+            nc.vector.tensor_tensor(f1[:].indirect(idx[:, halves[h]]), plus[h][:], minus[h][:], ADD)
+
+        f2 = sb.tile([P, T], F32, name="f2")
+        nc.vector.tensor_tensor(f2[:], f1[:], old_sb[:], ADD)
+
+        third = [sb.tile([P, HALF], F32, name="third%d" % h) for h in range(2)]
+        fourth = [sb.tile([P, HALF], F32, name="fourth%d" % h) for h in range(2)]
+        larger = [sb.tile([P, HALF], F32, name="larger%d" % h) for h in range(2)]
+        for h in range(2):
+            nc.vector.tensor_copy(third[h][:], f2[:].indirect(idx3[:, halves[h]]))
+            nc.scalar.activation(fourth[h][:], f2[:].indirect(idx4[:, halves[h]]), COPY)
+        for h in range(2):
+            nc.vector.tensor_tensor(larger[h][:], third[h][:], fourth[h][:], MAX)
+            nc.sync.dma_start(out=out[:, h * HALF : (h + 1) * HALF], in_=larger[h][:])

@@ -21,7 +21,9 @@ PACK = 4
 GROUP = 16
 HALF = I // 2
 KEY_LOADS = 2
-N_MM = 256
+QUARTER = T // 4
+MM_WIDTHS = (256, 256, 256, 128, 128)
+VECTOR_Q = 64
 
 
 def tile_attend_difference_lean_throughtwo_heads_kernel(
@@ -33,7 +35,7 @@ def tile_attend_difference_lean_throughtwo_heads_kernel(
         sb = ctx.enter_context(tc.tile_pool(name="sb", bufs=1))
         psum = ctx.enter_context(tc.psum_pool(name="psum", bufs=1))
 
-        k_scales = sb.tile([P, T], U8, name="k_scales", align_bytes=64)
+        k_scales = sb.tile([P, QUARTER], U8, name="k_scales", align_bytes=64)
         nc.vector.memset(k_scales[:].bitcast(I32), 0)
 
         q_raw = sb.tile([P, PACK, Q], F32, name="q_raw", tag="staged")
@@ -46,8 +48,8 @@ def tile_attend_difference_lean_throughtwo_heads_kernel(
         scale_rows = keys_scales[0].bitcast(I32)
         for quad in range(4):
             nc.sync.dma_start(
-                out=k_scales[32 * quad : 32 * quad + 4, :].bitcast(I32),
-                in_=scale_rows[4 * quad : 4 * quad + 4, :],
+                out=k_scales[32 * quad : 32 * quad + 16, :].bitcast(I32),
+                in_=scale_rows[4 * quad : 4 * quad + 4, :].rearrange("r (c n) -> c r n", c=4),
             )
         nc.sync.dma_start(out=k_words[1][:].bitcast(I32), in_=words[:, width:T])
 
@@ -55,14 +57,17 @@ def tile_attend_difference_lean_throughtwo_heads_kernel(
         idx2 = lists.tile([P, I // GROUP], U16, name="idx2")
         idx3 = lists.tile([P, I // GROUP], U16, name="idx3")
         idx4 = lists.tile([P, I // GROUP], U16, name="idx4")
-        nc.sync.dma_start(idx[:], offs)
         nc.sync.dma_start(idx2[:], offs2)
+        nc.sync.dma_start(idx[:], offs)
 
         f1 = sb.tile([P, T], F32, name="f1")
         nc.vector.memset(f1[:], 0.0)
 
         q_bf = sb.tile([P, Q, PACK], BF16, name="q_bf", align_bytes=64)
-        nc.vector.tensor_copy(out=q_bf[:], in_=q_raw[:].rearrange("p j q -> p q j"))
+        q_to = q_bf[:].rearrange("p (c i) j -> p c j i", i=4)
+        q_from = q_raw[:].rearrange("p j (c i) -> p c j i", i=4)
+        nc.vector.tensor_copy(out=q_to[:, 0 : VECTOR_Q // 4], in_=q_from[:, 0 : VECTOR_Q // 4])
+        nc.scalar.activation(q_to[:, VECTOR_Q // 4 :], q_from[:, VECTOR_Q // 4 :], COPY)
         q_words = sb.tile([P, Q], U32, name="q_words", align_bytes=64)
         q_scales = sb.tile([P, Q], U8, name="q_scales", align_bytes=64)
         nc.vector.quantize_mx(
@@ -75,16 +80,18 @@ def tile_attend_difference_lean_throughtwo_heads_kernel(
         nc.sync.dma_start(idx4[:], offs4)
 
         a = sb.tile([P, T], F32, name="a")
-        for m in range(T // N_MM):
-            cols = slice(m * N_MM, (m + 1) * N_MM)
-            c, first = divmod(m * N_MM, width)
-            bank = psum.tile([P, N_MM], F32, name="bank%d" % m)
+        for m, n in enumerate(MM_WIDTHS):
+            start = sum(MM_WIDTHS[:m])
+            cols = slice(start, start + n)
+            c, first = divmod(start, width)
+            quarter, within = divmod(start, QUARTER)
+            bank = psum.tile([P, n], F32, name="bank%d" % m)
             nc.tensor.matmul_mx(
                 out=bank[:],
                 lhsT=q_words[:].bitcast(FP8X4),
                 lhsT_scale=q_scales[:],
-                rhs=k_words[c][:, first : first + N_MM].bitcast(FP8X4),
-                rhs_scale=k_scales[:, cols],
+                rhs=k_words[c][:, first : first + n].bitcast(FP8X4),
+                rhs_scale=k_scales[4 * quarter : P, within : within + n],
                 start=True,
                 stop=True,
             )

from contextlib import ExitStack

import concourse.mybir as mybir

D, T, I, Q = 512, 1024, 512, 128
FLOPS = 2 * D * T * Q

F32 = mybir.dt.float32
BF16 = mybir.dt.bfloat16
I32 = mybir.dt.int32
U32 = mybir.dt.uint32
U16 = mybir.dt.uint16
U8 = mybir.dt.uint8
FP8X4 = mybir.dt.float8_e4m3fn_x4
COPY = mybir.ActivationFunctionType.Copy
ADD = mybir.AluOpType.add
MAX = mybir.AluOpType.max

P = 128
PACK = 4
GROUP = 16
HALF = I // 2
KEY_LOADS = 2
QUARTER = T // 4
MM_WIDTHS = (256, 256, 256, 128, 128)
VECTOR_Q = 64


def tile_attend_difference_lean_throughtwo_heads_kernel(
    tc, query, keys_words, keys_scales, old, offs, offs2, offs3, offs4, out
):
    nc = tc.nc
    with ExitStack() as ctx:
        lists = ctx.enter_context(tc.tile_pool(name="lists", bufs=1))
        sb = ctx.enter_context(tc.tile_pool(name="sb", bufs=1))
        psum = ctx.enter_context(tc.psum_pool(name="psum", bufs=1))

        k_scales = sb.tile([P, QUARTER], U8, name="k_scales", align_bytes=64)
        nc.vector.memset(k_scales[:].bitcast(I32), 0)

        q_raw = sb.tile([P, PACK, Q], F32, name="q_raw", tag="staged")
        nc.sync.dma_start(out=q_raw[:], in_=query.rearrange("(p j) q -> p j q", j=PACK))

        words = keys_words[0].rearrange("p t r -> p (t r)").bitcast(I32)
        width = T // KEY_LOADS
        k_words = [sb.tile([P, width], U32, name="k_words%d" % c, align_bytes=64) for c in range(KEY_LOADS)]
        nc.sync.dma_start(out=k_words[0][:].bitcast(I32), in_=words[:, 0:width])
        scale_rows = keys_scales[0].bitcast(I32)
        for quad in range(4):
            nc.sync.dma_start(
                out=k_scales[32 * quad : 32 * quad + 16, :].bitcast(I32),
                in_=scale_rows[4 * quad : 4 * quad + 4, :].rearrange("r (c n) -> c r n", c=4),
            )
        nc.sync.dma_start(out=k_words[1][:].bitcast(I32), in_=words[:, width:T])

        idx = lists.tile([P, I // GROUP], U16, name="idx")
        idx2 = lists.tile([P, I // GROUP], U16, name="idx2")
        idx3 = lists.tile([P, I // GROUP], U16, name="idx3")
        idx4 = lists.tile([P, I // GROUP], U16, name="idx4")
        nc.sync.dma_start(idx2[:], offs2)
        nc.sync.dma_start(idx[:], offs)

        f1 = sb.tile([P, T], F32, name="f1")
        nc.vector.memset(f1[:], 0.0)

        q_bf = sb.tile([P, Q, PACK], BF16, name="q_bf", align_bytes=64)
        q_to = q_bf[:].rearrange("p (c i) j -> p c j i", i=4)
        q_from = q_raw[:].rearrange("p j (c i) -> p c j i", i=4)
        nc.vector.tensor_copy(out=q_to[:, 0 : VECTOR_Q // 4], in_=q_from[:, 0 : VECTOR_Q // 4])
        nc.scalar.activation(q_to[:, VECTOR_Q // 4 :], q_from[:, VECTOR_Q // 4 :], COPY)
        q_words = sb.tile([P, Q], U32, name="q_words", align_bytes=64)
        q_scales = sb.tile([P, Q], U8, name="q_scales", align_bytes=64)
        nc.vector.quantize_mx(
            out=q_words[:].bitcast(FP8X4), scales=q_scales[:], in_=q_bf[:].rearrange("p q j -> p (q j)")
        )

        old_sb = sb.tile([P, T], F32, name="old_sb", tag="staged")
        nc.sync.dma_start(out=old_sb[:], in_=old)
        nc.sync.dma_start(idx3[:], offs3)
        nc.sync.dma_start(idx4[:], offs4)

        a = sb.tile([P, T], F32, name="a")
        for m, n in enumerate(MM_WIDTHS):
            start = sum(MM_WIDTHS[:m])
            cols = slice(start, start + n)
            c, first = divmod(start, width)
            quarter, within = divmod(start, QUARTER)
            bank = psum.tile([P, n], F32, name="bank%d" % m)
            nc.tensor.matmul_mx(
                out=bank[:],
                lhsT=q_words[:].bitcast(FP8X4),
                lhsT_scale=q_scales[:],
                rhs=k_words[c][:, first : first + n].bitcast(FP8X4),
                rhs_scale=k_scales[4 * quarter : P, within : within + n],
                start=True,
                stop=True,
            )
            if m % 2 == 0:
                nc.scalar.activation(a[:, cols], bank[:], COPY)
            else:
                nc.vector.tensor_copy(a[:, cols], bank[:])

        halves = [slice(h * HALF // GROUP, (h + 1) * HALF // GROUP) for h in range(2)]
        plus = [sb.tile([P, HALF], F32, name="plus%d" % h) for h in range(2)]
        minus = [sb.tile([P, HALF], F32, name="minus%d" % h) for h in range(2)]
        nc.vector.tensor_copy(plus[0][:], a[:].indirect(idx[:, halves[0]]))
        nc.scalar.activation(minus[0][:], a[:].indirect(idx2[:, halves[0]]), COPY, scale=-1.0)
        nc.scalar.activation(plus[1][:], a[:].indirect(idx[:, halves[1]]), COPY)
        nc.scalar.activation(minus[1][:], a[:].indirect(idx2[:, halves[1]]), COPY, scale=-1.0)
        for h in range(2):
            nc.vector.tensor_tensor(f1[:].indirect(idx[:, halves[h]]), plus[h][:], minus[h][:], ADD)

        f2 = sb.tile([P, T], F32, name="f2")
        nc.vector.tensor_tensor(f2[:], f1[:], old_sb[:], ADD)

        third = [sb.tile([P, HALF], F32, name="third%d" % h) for h in range(2)]
        fourth = [sb.tile([P, HALF], F32, name="fourth%d" % h) for h in range(2)]
        larger = [sb.tile([P, HALF], F32, name="larger%d" % h) for h in range(2)]
        for h in range(2):
            nc.vector.tensor_copy(third[h][:], f2[:].indirect(idx3[:, halves[h]]))
            nc.scalar.activation(fourth[h][:], f2[:].indirect(idx4[:, halves[h]]), COPY)
        for h in range(2):
            nc.vector.tensor_tensor(larger[h][:], third[h][:], fourth[h][:], MAX)
            nc.sync.dma_start(out=out[:, h * HALF : (h + 1) * HALF], in_=larger[h][:])
